import numpy as np
import ml_dtypes


def mxq(x, axis, fmt="e4m3"):
    dtype, down = {"e4m3": (ml_dtypes.float8_e4m3fn, 7), "e5m2": (ml_dtypes.float8_e5m2, 14)}[fmt]
    v = np.moveaxis(np.asarray(x, np.float32).astype(ml_dtypes.bfloat16).astype(np.float64), axis, -1)
    blocks = v.reshape(v.shape[:-1] + (-1, 32))
    amax = np.abs(blocks).max(-1, keepdims=True)
    byte = np.maximum(np.where(amax > 0, np.frexp(amax)[1] - 1 + 127, 0) - down, 1)
    scale = np.exp2(byte - 127.0)
    codes = (blocks / scale).astype(np.float32).astype(dtype).astype(np.float64)
    return np.moveaxis((codes * scale).reshape(v.shape), -1, axis)


WIDE = False


def mx_kscale(k):
    if not WIDE:
        return np.ones(k)
    levels = np.array([10, -10, 5, -5, 0])
    if k % 512:
        return np.exp2(np.random.permutation(np.resize(levels, k // 32))).repeat(32)
    a = np.empty((k // 512, 16))
    for p in range(k // 512):
        a[p, :8] = np.random.permutation(np.resize(levels, 8))
        for g in range(8):
            far = levels[np.abs(levels - a[p, g]) >= 10]
            a[p, g + 8] = far[np.random.randint(len(far))]
    return np.exp2(a.ravel()).repeat(32)


def f64(x):
    return np.asarray(x).astype(np.float64)


def striped(idx):
    return np.tile(idx.reshape(-1, 16).T, (8, 1)).astype(np.uint16)


def unstriped(offs):
    return offs[:16].T.reshape(-1).astype(np.int64)


E2M1 = np.array([0.0, 0.5, 1.0, 1.5, 2.0, 3.0, 4.0, 6.0, -0.0, -0.5, -1.0, -1.5, -2.0, -3.0, -4.0, -6.0])


def pack_weight(w, fmt):
    k, n = w.shape
    w = f64(np.asarray(w, np.float32).astype(ml_dtypes.bfloat16)).reshape(k // 32, 32, n)
    amax = np.abs(w).max(1)
    if fmt == "e4m3":
        byte = np.frexp(amax)[1] - 1 + 127 - 7
    else:
        mant, ex = np.frexp(amax / 6.0)
        byte = np.where(mant > 0.5, ex, ex - 1) + 127
    byte = np.clip(np.where(amax > 0, byte, 1), 1, 254)
    scaled = (w * np.exp2(127.0 - byte)[:, None, :]).reshape(k, n).astype(np.float32)
    by_word = np.ascontiguousarray(scaled.reshape(k // 512, 128, 4, n).transpose(0, 1, 3, 2))
    if fmt == "e4m3":
        words = by_word.astype(ml_dtypes.float8_e4m3fn).view(np.uint8)
    else:
        c = by_word.astype(ml_dtypes.float4_e2m1fn).view(np.uint8) & 0xF
        words = (c[..., 0::2] | (c[..., 1::2] << 4)).reshape(k // 512, 128, 2 * n)
    return np.ascontiguousarray(words), np.ascontiguousarray(byte.astype(np.uint8).reshape(k // 512, 16, n))


def unpack_weight(words, scales, fmt):
    g, _, n = scales.shape
    words = np.ascontiguousarray(words).reshape(g, 128, n, -1)
    if fmt == "e4m3":
        vals = words.view(ml_dtypes.float8_e4m3fn).astype(np.float64)
    else:
        nib = np.empty((g, 128, n, 4), np.uint8)
        nib[..., 0::2] = words & 0xF
        nib[..., 1::2] = words >> 4
        vals = E2M1[nib]
    vals = vals * np.repeat(np.exp2(scales.astype(np.float64) - 127.0), 8, axis=1)[..., None]
    return vals.transpose(0, 1, 3, 2).reshape(g * 512, n)


def gelu(v):
    return 0.5 * v * (1.0 + np.tanh(np.sqrt(2.0 / np.pi) * (v + 0.044715 * v**3)))


K, H, N, T, S, P = 1536, 512, 768, 4096, 1024, 512

def setup_inputs():
    n = np.random.standard_normal
    s = mx_kscale(K)[:, None]
    u = mx_kscale(H)[:, None]
    tab_words, tab_scales = pack_weight(n((K, T)) * s, "e4m3")
    w2_words, w2_scales = pack_weight(0.75 * n((K, H)) / np.sqrt(K) / s * u.T, "e4m3")
    w4_words, w4_scales = pack_weight(n((H, N)) / np.sqrt(H) / u, "e2m1")
    return {
        "tab_words": tab_words, "tab_scales": tab_scales,
        "offs": striped(np.random.permutation(T)[:S]),
        "pos1": striped(np.random.permutation(S)[:P]),
        "pos2": striped(np.random.permutation(S)[:P]),
        "w1": (1.4 * n((K, H)) / np.sqrt(K) / s).astype(np.float32),
        "b1": (0.5 * n(H)).astype(np.float32),
        "w2_words": w2_words, "w2_scales": w2_scales,
        "thr": n(H).astype(np.float32),
        "dist": (1.8 * n((H, P)) * u).astype(np.float32),
        "w3": (n((H, N)) / np.sqrt(H) / u).astype(np.float32),
        "b3": (0.5 * n(N)).astype(np.float32),
        "w4_words": w4_words, "w4_scales": w4_scales,
    }

def reference(tab_words, tab_scales, offs, pos1, pos2, w1, b1, w2_words, w2_scales,
              thr, dist, w3, b3, w4_words, w4_scales):
    v = unpack_weight(tab_words, tab_scales, "e4m3")[:, unstriped(offs)]
    pre = (mxq(f64(w1), 0, "e4m3").T @ v) + f64(b1)[:, None]
    h = pre / (1.0 + np.exp(-pre))
    g = unpack_weight(w2_words, w2_scales, "e4m3").T @ v
    a = 1.0 / (1.0 + np.exp(-(h[:, unstriped(pos1)] + f64(thr)[:, None])))
    x = a * f64(dist) + g[:, unstriped(pos2)]
    xq = mxq(x, 0, "e4m3")
    y3 = (mxq(f64(w3), 0, "e4m3").T @ xq) + f64(b3)[:, None]
    y4 = unpack_weight(w4_words, w4_scales, "e2m1").T @ xq
    return np.maximum(y3, y4)

@@ -1,0 +1,269 @@
+from contextlib import ExitStack
+
+import concourse.mybir as mybir
+
+K, H, N, T, S, M = 1536, 512, 768, 4096, 1024, 512
+FLOPS = 2 * (2 * K * H * S + 2 * H * N * M)
+
+F32 = mybir.dt.float32
+BF16 = mybir.dt.bfloat16
+I32 = mybir.dt.int32
+U32 = mybir.dt.uint32
+U16 = mybir.dt.uint16
+U8 = mybir.dt.uint8
+FP8X4 = mybir.dt.float8_e4m3fn_x4
+FP4X4 = mybir.dt.float4_e2m1fn_x4
+ACT = mybir.ActivationFunctionType
+ALU = mybir.AluOpType
+
+P = 128
+PACK = 4
+PASSES = K // (P * PACK)
+BANK = 512
+HALVES = S // BANK
+QUADS = 4
+ROWS = 4
+CHUNK = 256
+CHUNKS = M // CHUNK
+N_TILES = N // P
+VEC_COLS = 84
+
+
+def tile_list_introduction_scores_kernel(
+    tc, tab_words, tab_scales, offs, pos1, pos2, w1, b1, w2_words, w2_scales,
+    thr, dist, w3, b3, w4_words, w4_scales, out,
+):
+    nc = tc.nc
+    with ExitStack() as ctx:
+        keep = ctx.enter_context(tc.tile_pool(name="keep", bufs=1))
+        ring = ctx.enter_context(tc.tile_pool(name="ring", bufs=4))
+        psum = ctx.enter_context(tc.psum_pool(name="psum", bufs=1))
+
+        def bank(b, name):
+            return psum.tile([P, BANK], F32, name=name, tag="bank%d" % b)
+
+        offs_sb = keep.tile([P, S // 16], U16, name="offs_sb")
+        pos1_sb = keep.tile([P, M // 16], U16, name="pos1_sb")
+        pos2_sb = keep.tile([P, M // 16], U16, name="pos2_sb")
+        tab = [keep.tile([P, T], I32, name="tab%d" % a) for a in range(PASSES)]
+        tab_sc = keep.tile([P, T // 4], I32, name="tab_sc")
+        w2_raw = keep.tile([P, PASSES, H], I32, name="w2_raw")
+        w2_sc_raw = keep.tile([P, H // 4], I32, name="w2_sc_raw")
+        w1_raw = [keep.tile([P, PACK, H], F32, name="w1_raw%d" % a) for a in range(PASSES)]
+        b1_sb = keep.tile([P, PACK], F32, name="b1_sb", tag="gate")
+        thr_sb = keep.tile([P, PACK], F32, name="thr_sb")
+        b3_sb = keep.tile([P, N_TILES], F32, name="b3_sb")
+        w3_raw = keep.tile([P, PACK, N], F32, name="w3_raw")
+        dist_sb = keep.tile([P, PACK, M], F32, name="dist_sb")
+        w4_sb = keep.tile([P, N // 2], I32, name="w4_sb", align_bytes=64)
+        w4_sc = keep.tile([P, N // 4], I32, name="w4_sc", align_bytes=64)
+
+        nc.vector.memset(tab_sc[:], 0)
+        nc.vector.memset(w2_sc_raw[:], 0)
+        nc.vector.memset(w4_sc[:], 0)
+
+        def load_scales(queue, tile, scales):
+            passes = scales.shape[0]
+            words = scales.bitcast(I32)
+            for q in range(QUADS):
+                queue.dma_start(
+                    out=tile[32 * q : 32 * q + ROWS * passes, :],
+                    in_=words[:, ROWS * q : ROWS * (q + 1), :],
+                )
+
+        def load_table(a):
+            nc.sync.dma_start(out=tab[a][:], in_=tab_words[a].rearrange("p t i -> p (t i)").bitcast(I32))
+
+        load_table(0)
+        load_scales(nc.sync, tab_sc, tab_scales)
+        nc.sync.dma_start(out=offs_sb[:], in_=offs)
+        nc.sync.dma_start(out=w2_raw[:], in_=w2_words.rearrange("a p c i -> p a (c i)").bitcast(I32))
+        load_scales(nc.sync, w2_sc_raw, w2_scales)
+        load_table(1)
+        load_table(2)
+        for a in range(PASSES):
+            nc.sync.dma_start(
+                out=w1_raw[a][:], in_=w1[a * 512 : (a + 1) * 512, :].rearrange("(p j) c -> p j c", j=PACK)
+            )
+        nc.sync.dma_start(out=b1_sb[:], in_=b1.rearrange("(p t) -> p t", t=PACK))
+        nc.sync.dma_start(out=pos2_sb[:], in_=pos2)
+        nc.sync.dma_start(out=w3_raw[:], in_=w3.rearrange("(p j) n -> p j n", j=PACK))
+        nc.sync.dma_start(out=pos1_sb[:], in_=pos1)
+        nc.sync.dma_start(out=thr_sb[:], in_=thr.rearrange("(p t) -> p t", t=PACK))
+        nc.sync.dma_start(out=dist_sb[:], in_=dist.rearrange("(p t) m -> p t m", t=PACK))
+        nc.sync.dma_start(out=w4_sb[:], in_=w4_words[0].bitcast(I32))
+        load_scales(nc.sync, w4_sc, w4_scales)
+        with nc.allow_non_contiguous_dma(reason="one bias value a partition"):
+            nc.sync.dma_start(out=b3_sb[:], in_=b3.rearrange("(c p) -> p c", p=P))
+
+        v = [[keep.tile([P, BANK], U32, name="v%d_%d" % (a, s), align_bytes=64) for s in range(HALVES)] for a in range(PASSES)]
+        v_sc = keep.tile([P, S], U8, name="v_sc", align_bytes=64)
+
+        def gather_table(a):
+            for s in range(HALVES):
+                cols = offs_sb[:, s * BANK // 16 : (s + 1) * BANK // 16]
+                nc.vector.tensor_copy(out=v[a][s][:], in_=tab[a][:].bitcast(U32).indirect(cols))
+
+        gather_table(0)
+        nc.vector.tensor_copy(out=v_sc[:], in_=tab_sc[:].bitcast(U8).indirect(offs_sb[:]))
+
+        w2_q = keep.tile([P, PASSES, H], I32, name="w2_q", align_bytes=64)
+        w2_sc = keep.tile([P, H], U8, name="w2_sc", align_bytes=64)
+        nc.vector.tensor_copy(
+            out=w2_q[:].rearrange("p a (t m) -> p a m t", t=PACK),
+            in_=w2_raw[:].rearrange("p a (m t) -> p a m t", t=PACK),
+        )
+        nc.vector.tensor_copy(
+            out=w2_sc[:].rearrange("p (t m) -> p t m", t=PACK),
+            in_=w2_sc_raw[:].bitcast(U8).rearrange("p (m t) -> p t m", t=PACK),
+        )
+        gather_table(1)
+        gather_table(2)
+
+        def first_stage(acc, codes, scales, t, s):
+            for a in range(PASSES):
+                nc.tensor.matmul_mx(
+                    out=acc[:],
+                    lhsT=codes(a, t),
+                    lhsT_scale=scales(a, t),
+                    rhs=v[a][s][:].bitcast(FP8X4),
+                    rhs_scale=v_sc[ROWS * a :, s * BANK : (s + 1) * BANK],
+                    start=(a == 0),
+                    stop=(a == PASSES - 1),
+                )
+
+        g = [keep.tile([P, S], F32, name="g%d" % t) for t in range(PACK)]
+        for s in range(HALVES):
+            for t in range(PACK):
+                acc = bank(PACK * s + t, "g_acc")
+                first_stage(
+                    acc,
+                    lambda a, t: w2_q[:, a, t * P : (t + 1) * P].bitcast(FP8X4),
+                    lambda a, t: w2_sc[ROWS * a :, t * P : (t + 1) * P],
+                    t, s,
+                )
+                nc.scalar.copy(out=g[t][:, s * BANK : (s + 1) * BANK], in_=acc[:])
+
+        w1_q = [keep.tile([P, H], U32, name="w1_q%d" % a, align_bytes=64) for a in range(PASSES)]
+        w1_sc = [keep.tile([P, H], U8, name="w1_sc%d" % a, align_bytes=64) for a in range(PASSES)]
+        for a in range(PASSES):
+            grouped = keep.tile([P, H * PACK], BF16, name="w1_bf%d" % a, tag="w1_bf%d" % a, align_bytes=64)
+            dst = grouped[:].rearrange("p (t m j) -> p m j t", t=PACK, j=PACK)
+            src = w1_raw[a][:].rearrange("p j (m t) -> p m j t", t=PACK)
+            if a < PASSES - 1:
+                nc.vector.tensor_copy(out=dst, in_=src)
+                nc.vector.quantize_mx(out=w1_q[a][:].bitcast(FP8X4), scales=w1_sc[a][:], in_=grouped[:])
+            else:
+                nc.vector.tensor_copy(out=dst[:, :VEC_COLS], in_=src[:, :VEC_COLS])
+                nc.scalar.copy(out=dst[:, VEC_COLS:], in_=src[:, VEC_COLS:])
+                for t in range(PACK):
+                    nc.vector.quantize_mx(
+                        out=w1_q[a][:, t * P : (t + 1) * P].bitcast(FP8X4),
+                        scales=w1_sc[a][:, t * P : (t + 1) * P],
+                        in_=grouped[:, t * H : (t + 1) * H],
+                    )
+
+        h = [keep.tile([P, S], F32, name="h%d" % t) for t in range(PACK)]
+        for t in range(PACK):
+            for s in range(HALVES):
+                acc = bank(HALVES * t + s, "h_acc")
+                first_stage(
+                    acc,
+                    lambda a, t: w1_q[a][:, t * P : (t + 1) * P].bitcast(FP8X4),
+                    lambda a, t: w1_sc[a][:, t * P : (t + 1) * P],
+                    t, s,
+                )
+                nc.scalar.activation(
+                    out=h[t][:, s * BANK : (s + 1) * BANK], in_=acc[:], func=ACT.Silu, bias=b1_sb[:, t : t + 1]
+                )
+
+        picked = keep.tile([P, PACK, M], F32, name="picked", tag="w1_bf%d" % (PASSES - 1), align_bytes=64)
+        for t in range(PACK):
+            nc.vector.tensor_copy(out=picked[:, t, :], in_=g[t][:].indirect(pos2_sb[:]))
+
+        w3_bf = keep.tile([P, N * PACK], BF16, name="w3_bf", align_bytes=64)
+        w3_q = keep.tile([P, N], U32, name="w3_q", align_bytes=64)
+        w3_sc = keep.tile([P, N], U8, name="w3_sc", align_bytes=64)
+        nc.vector.tensor_copy(
+            out=w3_bf[:].rearrange("p (c i j) -> p c j i", i=4, j=PACK),
+            in_=w3_raw[:].rearrange("p j (c i) -> p c j i", i=4),
+        )
+        for u in range(2):
+            nc.vector.quantize_mx(
+                out=w3_q[:, u * N // 2 : (u + 1) * N // 2].bitcast(FP8X4),
+                scales=w3_sc[:, u * N // 2 : (u + 1) * N // 2],
+                in_=w3_bf[:, u * N * 2 : (u + 1) * N * 2],
+            )
+
+        gate = keep.tile([P, PACK, M], F32, name="gate", tag="gate")
+        for c in range(CHUNKS):
+            cols = slice(c * CHUNK, (c + 1) * CHUNK)
+            for t in range(PACK):
+                nc.scalar.activation(
+                    out=gate[:, t, cols],
+                    in_=h[t][:].indirect(pos1_sb[:, c * CHUNK // 16 : (c + 1) * CHUNK // 16]),
+                    func=ACT.Sigmoid,
+                    bias=thr_sb[:, t : t + 1],
+                )
+        x_qs, x_scs = [], []
+        for c in range(CHUNKS):
+            cols = slice(c * CHUNK, (c + 1) * CHUNK)
+            for t in range(PACK):
+                nc.vector.tensor_tensor(out=gate[:, t, cols], in0=gate[:, t, cols], in1=dist_sb[:, t, cols], op=ALU.mult)
+            x_bf = keep.tile([P, CHUNK * PACK], BF16, name="x_bf%d" % c, align_bytes=64)
+            x_q = keep.tile([P, CHUNK], U32, name="x_q%d" % c, align_bytes=64)
+            x_sc = keep.tile([P, CHUNK], U8, name="x_sc%d" % c, align_bytes=64)
+            nc.vector.tensor_tensor(
+                out=x_bf[:].rearrange("p (c i t) -> p c t i", i=2, t=PACK),
+                in0=gate[:, :, cols].rearrange("p t (c i) -> p c t i", i=2),
+                in1=picked[:, :, cols].rearrange("p t (c i) -> p c t i", i=2),
+                op=ALU.add,
+            )
+            nc.vector.quantize_mx(out=x_q[:].bitcast(FP8X4), scales=x_sc[:], in_=x_bf[:])
+            x_qs.append(x_q)
+            x_scs.append(x_sc)
+
+        for c in range(CHUNKS):
+            cols = slice(c * CHUNK, (c + 1) * CHUNK)
+            x_q, x_sc = x_qs[c], x_scs[c]
+            for pair in range(N_TILES // 2):
+                first = 2 * (c * (N_TILES // 2) + pair)
+                y4 = bank(first % 8, "y4")
+                y3 = bank((first + 1) % 8, "y3")
+                for e in range(2):
+                    n = 2 * pair + e
+                    nc.tensor.matmul_mx(
+                        out=y3[:, e * CHUNK : (e + 1) * CHUNK],
+                        lhsT=w3_q[:, n * P : (n + 1) * P].bitcast(FP8X4),
+                        lhsT_scale=w3_sc[:, n * P : (n + 1) * P],
+                        rhs=x_q[:].bitcast(FP8X4),
+                        rhs_scale=x_sc[:],
+                        start=True,
+                        stop=True,
+                    )
+                for e in range(2):
+                    n = 2 * pair + e
+                    nc.tensor.matmul_mx(
+                        out=y4[:, e * CHUNK : (e + 1) * CHUNK],
+                        lhsT=w4_sb[:].bitcast(U8)[:, 2 * n * P : 2 * (n + 1) * P].bitcast(FP4X4),
+                        lhsT_scale=w4_sc[:].bitcast(U8)[:, n * P : (n + 1) * P],
+                        rhs=x_q[:].bitcast(FP8X4),
+                        rhs_scale=x_sc[:],
+                        start=True,
+                        stop=True,
+                    )
+                y3_sb = ring.tile([P, BANK], F32, name="y3_sb")
+                for e in range(2):
+                    n = 2 * pair + e
+                    nc.scalar.activation(
+                        out=y3_sb[:, e * CHUNK : (e + 1) * CHUNK],
+                        in_=y3[:, e * CHUNK : (e + 1) * CHUNK],
+                        func=ACT.Identity,
+                        bias=b3_sb[:, n : n + 1],
+                    )
+                best = ring.tile([P, BANK], F32, name="best")
+                nc.vector.tensor_tensor(out=best[:], in0=y4[:], in1=y3_sb[:], op=ALU.max)
+                nc.sync.dma_start(
+                    out=out[2 * pair * P : 2 * (pair + 1) * P, cols].rearrange("(e p) m -> p e m", p=P),
+                    in_=best[:].rearrange("p (e m) -> p e m", e=2),
+                )

@@ -26,7 +26,7 @@ ROWS = 4
 CHUNK = 256
 CHUNKS = M // CHUNK
 N_TILES = N // P
-VEC_COLS = 84
+PAIRS = N_TILES // 2
 
 
 def tile_list_introduction_scores_kernel(
@@ -58,15 +58,15 @@ def tile_list_introduction_scores_kernel(
         w4_sb = keep.tile([P, N // 2], I32, name="w4_sb", align_bytes=64)
         w4_sc = keep.tile([P, N // 4], I32, name="w4_sc", align_bytes=64)
 
-        nc.vector.memset(tab_sc[:], 0)
         nc.vector.memset(w2_sc_raw[:], 0)
+        nc.vector.memset(tab_sc[:], 0)
         nc.vector.memset(w4_sc[:], 0)
 
-        def load_scales(queue, tile, scales):
+        def load_scales(tile, scales, quads):
             passes = scales.shape[0]
             words = scales.bitcast(I32)
-            for q in range(QUADS):
-                queue.dma_start(
+            for q in quads:
+                nc.sync.dma_start(
                     out=tile[32 * q : 32 * q + ROWS * passes, :],
                     in_=words[:, ROWS * q : ROWS * (q + 1), :],
                 )
@@ -75,10 +75,12 @@ def tile_list_introduction_scores_kernel(
             nc.sync.dma_start(out=tab[a][:], in_=tab_words[a].rearrange("p t i -> p (t i)").bitcast(I32))
 
         load_table(0)
-        load_scales(nc.sync, tab_sc, tab_scales)
         nc.sync.dma_start(out=offs_sb[:], in_=offs)
+        load_scales(tab_sc, tab_scales, (2, 3))
+        load_scales(w2_sc_raw, w2_scales, (2, 3))
+        load_scales(tab_sc, tab_scales, (0, 1))
         nc.sync.dma_start(out=w2_raw[:], in_=w2_words.rearrange("a p c i -> p a (c i)").bitcast(I32))
-        load_scales(nc.sync, w2_sc_raw, w2_scales)
+        load_scales(w2_sc_raw, w2_scales, (0, 1))
         load_table(1)
         load_table(2)
         for a in range(PASSES):
@@ -92,31 +94,35 @@ def tile_list_introduction_scores_kernel(
         nc.sync.dma_start(out=thr_sb[:], in_=thr.rearrange("(p t) -> p t", t=PACK))
         nc.sync.dma_start(out=dist_sb[:], in_=dist.rearrange("(p t) m -> p t m", t=PACK))
         nc.sync.dma_start(out=w4_sb[:], in_=w4_words[0].bitcast(I32))
-        load_scales(nc.sync, w4_sc, w4_scales)
+        load_scales(w4_sc, w4_scales, range(QUADS))
         with nc.allow_non_contiguous_dma(reason="one bias value a partition"):
             nc.sync.dma_start(out=b3_sb[:], in_=b3.rearrange("(c p) -> p c", p=P))
 
         v = [[keep.tile([P, BANK], U32, name="v%d_%d" % (a, s), align_bytes=64) for s in range(HALVES)] for a in range(PASSES)]
-        v_sc = keep.tile([P, S], U8, name="v_sc", align_bytes=64)
+        v_sc = [keep.tile([P, BANK], U8, name="v_sc%d" % s, align_bytes=64) for s in range(HALVES)]
 
         def gather_table(a):
             for s in range(HALVES):
                 cols = offs_sb[:, s * BANK // 16 : (s + 1) * BANK // 16]
                 nc.vector.tensor_copy(out=v[a][s][:], in_=tab[a][:].bitcast(U32).indirect(cols))
 
+
         gather_table(0)
-        nc.vector.tensor_copy(out=v_sc[:], in_=tab_sc[:].bitcast(U8).indirect(offs_sb[:]))
+        for s in range(HALVES):
+            cols = offs_sb[:, s * BANK // 16 : (s + 1) * BANK // 16]
+            nc.vector.tensor_copy(out=v_sc[s][:], in_=tab_sc[:].bitcast(U8).indirect(cols))
 
         w2_q = keep.tile([P, PASSES, H], I32, name="w2_q", align_bytes=64)
         w2_sc = keep.tile([P, H], U8, name="w2_sc", align_bytes=64)
         nc.vector.tensor_copy(
-            out=w2_q[:].rearrange("p a (t m) -> p a m t", t=PACK),
-            in_=w2_raw[:].rearrange("p a (m t) -> p a m t", t=PACK),
-        )
-        nc.vector.tensor_copy(
             out=w2_sc[:].rearrange("p (t m) -> p t m", t=PACK),
             in_=w2_sc_raw[:].bitcast(U8).rearrange("p (m t) -> p t m", t=PACK),
         )
+        for a in range(PASSES):
+            nc.vector.tensor_copy(
+                out=w2_q[:, a, :].rearrange("p (t m) -> p m t", t=PACK),
+                in_=w2_raw[:, a, :].rearrange("p (m t) -> p m t", t=PACK),
+            )
         gather_table(1)
         gather_table(2)
 
@@ -127,7 +133,7 @@ def tile_list_introduction_scores_kernel(
                     lhsT=codes(a, t),
                     lhsT_scale=scales(a, t),
                     rhs=v[a][s][:].bitcast(FP8X4),
-                    rhs_scale=v_sc[ROWS * a :, s * BANK : (s + 1) * BANK],
+                    rhs_scale=v_sc[s][ROWS * a :, :],
                     start=(a == 0),
                     stop=(a == PASSES - 1),
                 )
@@ -144,40 +150,67 @@ def tile_list_introduction_scores_kernel(
                 )
                 nc.scalar.copy(out=g[t][:, s * BANK : (s + 1) * BANK], in_=acc[:])
 
+        w1_bf = [
+            [
+                keep.tile([P, 2 * H], BF16, name="w1_bf%d_%d" % (a, u), tag="w1_bf%d_%d" % (a, u), align_bytes=64)
+                for u in range(2)
+            ]
+            for a in range(PASSES)
+        ]
         w1_q = [keep.tile([P, H], U32, name="w1_q%d" % a, align_bytes=64) for a in range(PASSES)]
         w1_sc = [keep.tile([P, H], U8, name="w1_sc%d" % a, align_bytes=64) for a in range(PASSES)]
-        for a in range(PASSES):
-            grouped = keep.tile([P, H * PACK], BF16, name="w1_bf%d" % a, tag="w1_bf%d" % a, align_bytes=64)
-            dst = grouped[:].rearrange("p (t m j) -> p m j t", t=PACK, j=PACK)
-            src = w1_raw[a][:].rearrange("p j (m t) -> p m j t", t=PACK)
-            if a < PASSES - 1:
-                nc.vector.tensor_copy(out=dst, in_=src)
-                nc.vector.quantize_mx(out=w1_q[a][:].bitcast(FP8X4), scales=w1_sc[a][:], in_=grouped[:])
-            else:
-                nc.vector.tensor_copy(out=dst[:, :VEC_COLS], in_=src[:, :VEC_COLS])
-                nc.scalar.copy(out=dst[:, VEC_COLS:], in_=src[:, VEC_COLS:])
-                for t in range(PACK):
-                    nc.vector.quantize_mx(
-                        out=w1_q[a][:, t * P : (t + 1) * P].bitcast(FP8X4),
-                        scales=w1_sc[a][:, t * P : (t + 1) * P],
-                        in_=grouped[:, t * H : (t + 1) * H],
-                    )
+
+        def w1_plane(a, lo, hi):
+            if a == 1 and lo >= 2:
+                return w1_sc[2][ROWS:, (lo - 2) * P : (hi - 2) * P]
+            return w1_sc[a][:, lo * P : hi * P]
+
+        def round_w1(a, u):
+            dst = w1_bf[a][u][:].rearrange("p (e m j) -> p m j e", e=2, j=PACK)
+            src = w1_raw[a][:].rearrange("p j (m u e) -> p u m j e", u=2, e=2)
+            nc.vector.tensor_copy(out=dst, in_=src[:, u])
+
+        def quantise_w1(a, lo, hi):
+            nc.vector.quantize_mx(
+                out=w1_q[a][:, lo * P : hi * P].bitcast(FP8X4),
+                scales=w1_plane(a, lo, hi),
+                in_=w1_bf[a][lo // 2][:, (lo % 2) * H : (lo % 2 + hi - lo) * H],
+            )
 
         h = [keep.tile([P, S], F32, name="h%d" % t) for t in range(PACK)]
-        for t in range(PACK):
+
+        def make_h(t):
             for s in range(HALVES):
                 acc = bank(HALVES * t + s, "h_acc")
                 first_stage(
                     acc,
                     lambda a, t: w1_q[a][:, t * P : (t + 1) * P].bitcast(FP8X4),
-                    lambda a, t: w1_sc[a][:, t * P : (t + 1) * P],
+                    lambda a, t: w1_plane(a, t, t + 1),
                     t, s,
                 )
                 nc.scalar.activation(
                     out=h[t][:, s * BANK : (s + 1) * BANK], in_=acc[:], func=ACT.Silu, bias=b1_sb[:, t : t + 1]
                 )
 
-        picked = keep.tile([P, PACK, M], F32, name="picked", tag="w1_bf%d" % (PASSES - 1), align_bytes=64)
+        round_w1(0, 0)
+        round_w1(0, 1)
+        quantise_w1(0, 0, 2)
+        quantise_w1(0, 2, 4)
+        round_w1(1, 0)
+        round_w1(1, 1)
+        quantise_w1(1, 0, 2)
+        round_w1(2, 0)
+        quantise_w1(2, 0, 1)
+        quantise_w1(2, 1, 2)
+        round_w1(2, 1)
+        for t in range(2):
+            make_h(t)
+            quantise_w1(2, t + 2, t + 3)
+            quantise_w1(1, t + 2, t + 3)
+        make_h(2)
+        make_h(3)
+
+        picked = keep.tile([P, PACK, M], F32, name="picked", tag="w1_bf1_1", align_bytes=64)
         for t in range(PACK):
             nc.vector.tensor_copy(out=picked[:, t, :], in_=g[t][:].indirect(pos2_sb[:]))
 
@@ -206,34 +239,51 @@ def tile_list_introduction_scores_kernel(
                     bias=thr_sb[:, t : t + 1],
                 )
         x_qs, x_scs = [], []
+        prod = keep.tile([P, PACK, CHUNK], F32, name="prod")
         for c in range(CHUNKS):
             cols = slice(c * CHUNK, (c + 1) * CHUNK)
-            for t in range(PACK):
-                nc.vector.tensor_tensor(out=gate[:, t, cols], in0=gate[:, t, cols], in1=dist_sb[:, t, cols], op=ALU.mult)
+            for t in range(PACK - 1):
+                nc.vector.tensor_tensor(out=prod[:, t, :], in0=gate[:, t, cols], in1=dist_sb[:, t, cols], op=ALU.mult)
             x_bf = keep.tile([P, CHUNK * PACK], BF16, name="x_bf%d" % c, align_bytes=64)
             x_q = keep.tile([P, CHUNK], U32, name="x_q%d" % c, align_bytes=64)
             x_sc = keep.tile([P, CHUNK], U8, name="x_sc%d" % c, align_bytes=64)
-            nc.vector.tensor_tensor(
-                out=x_bf[:].rearrange("p (c i t) -> p c t i", i=2, t=PACK),
-                in0=gate[:, :, cols].rearrange("p t (c i) -> p c t i", i=2),
-                in1=picked[:, :, cols].rearrange("p t (c i) -> p c t i", i=2),
-                op=ALU.add,
-            )
-            nc.vector.quantize_mx(out=x_q[:].bitcast(FP8X4), scales=x_sc[:], in_=x_bf[:])
+            parts = [slice(c * CHUNK + d * P, c * CHUNK + (d + 1) * P) for d in range(2)]
+            for d, part in enumerate(parts):
+                nc.vector.tensor_tensor(
+                    out=prod[:, PACK - 1, d * P : (d + 1) * P],
+                    in0=gate[:, PACK - 1, part],
+                    in1=dist_sb[:, PACK - 1, part],
+                    op=ALU.mult,
+                )
+            for d, part in enumerate(parts):
+                nc.vector.tensor_tensor(
+                    out=x_bf[:, d * P * PACK : (d + 1) * P * PACK].rearrange("p (c i t) -> p c t i", i=2, t=PACK),
+                    in0=prod[:, :, d * P : (d + 1) * P].rearrange("p t (c i) -> p c t i", i=2),
+                    in1=picked[:, :, part].rearrange("p t (c i) -> p c t i", i=2),
+                    op=ALU.add,
+                )
+            for d in range(2):
+                nc.vector.quantize_mx(
+                    out=x_q[:, d * P : (d + 1) * P].bitcast(FP8X4),
+                    scales=x_sc[:, d * P : (d + 1) * P],
+                    in_=x_bf[:, d * P * PACK : (d + 1) * P * PACK],
+                )
             x_qs.append(x_q)
             x_scs.append(x_sc)
 
         for c in range(CHUNKS):
             cols = slice(c * CHUNK, (c + 1) * CHUNK)
             x_q, x_sc = x_qs[c], x_scs[c]
-            for pair in range(N_TILES // 2):
-                first = 2 * (c * (N_TILES // 2) + pair)
-                y4 = bank(first % 8, "y4")
-                y3 = bank((first + 1) % 8, "y3")
+            y3s, y4s = [], []
+            for pair in range(PAIRS):
+                y3s.append(bank((c * PAIRS + pair) % 4, "y3"))
+                y4s.append(bank(4 + (c * PAIRS + pair) % 4, "y4"))
+
+            def product3(pair):
                 for e in range(2):
                     n = 2 * pair + e
                     nc.tensor.matmul_mx(
-                        out=y3[:, e * CHUNK : (e + 1) * CHUNK],
+                        out=y3s[pair][:, e * CHUNK : (e + 1) * CHUNK],
                         lhsT=w3_q[:, n * P : (n + 1) * P].bitcast(FP8X4),
                         lhsT_scale=w3_sc[:, n * P : (n + 1) * P],
                         rhs=x_q[:].bitcast(FP8X4),
@@ -241,10 +291,12 @@ def tile_list_introduction_scores_kernel(
                         start=True,
                         stop=True,
                     )
+
+            def product4(pair):
                 for e in range(2):
                     n = 2 * pair + e
                     nc.tensor.matmul_mx(
-                        out=y4[:, e * CHUNK : (e + 1) * CHUNK],
+                        out=y4s[pair][:, e * CHUNK : (e + 1) * CHUNK],
                         lhsT=w4_sb[:].bitcast(U8)[:, 2 * n * P : 2 * (n + 1) * P].bitcast(FP4X4),
                         lhsT_scale=w4_sc[:].bitcast(U8)[:, n * P : (n + 1) * P],
                         rhs=x_q[:].bitcast(FP8X4),
@@ -252,17 +304,24 @@ def tile_list_introduction_scores_kernel(
                         start=True,
                         stop=True,
                     )
+
+            product3(0)
+            for pair in range(PAIRS):
+                if pair + 1 < PAIRS:
+                    product3(pair + 1)
+                product4(pair)
+            for pair in range(PAIRS):
                 y3_sb = ring.tile([P, BANK], F32, name="y3_sb")
                 for e in range(2):
                     n = 2 * pair + e
                     nc.scalar.activation(
                         out=y3_sb[:, e * CHUNK : (e + 1) * CHUNK],
-                        in_=y3[:, e * CHUNK : (e + 1) * CHUNK],
+                        in_=y3s[pair][:, e * CHUNK : (e + 1) * CHUNK],
                         func=ACT.Identity,
                         bias=b3_sb[:, n : n + 1],
                     )
-                best = ring.tile([P, BANK], F32, name="best")
-                nc.vector.tensor_tensor(out=best[:], in0=y4[:], in1=y3_sb[:], op=ALU.max)
+                best = ring.tile([P, BANK], F32, name="best", bufs=6)
+                nc.vector.tensor_tensor(out=best[:], in0=y4s[pair][:], in1=y3_sb[:], op=ALU.max)
                 nc.sync.dma_start(
                     out=out[2 * pair * P : 2 * (pair + 1) * P, cols].rearrange("(e p) m -> p e m", p=P),
                     in_=best[:].rearrange("p (e m) -> p e m", e=2),

from contextlib import ExitStack

import concourse.mybir as mybir

K, H, N, T, S, M = 1536, 512, 768, 4096, 1024, 512
FLOPS = 2 * (2 * K * H * S + 2 * H * N * M)

F32 = mybir.dt.float32
BF16 = mybir.dt.bfloat16
I32 = mybir.dt.int32
U32 = mybir.dt.uint32
U16 = mybir.dt.uint16
U8 = mybir.dt.uint8
FP8X4 = mybir.dt.float8_e4m3fn_x4
FP4X4 = mybir.dt.float4_e2m1fn_x4
ACT = mybir.ActivationFunctionType
ALU = mybir.AluOpType

P = 128
PACK = 4
PASSES = K // (P * PACK)
BANK = 512
HALVES = S // BANK
QUADS = 4
ROWS = 4
CHUNK = 256
CHUNKS = M // CHUNK
N_TILES = N // P
PAIRS = N_TILES // 2


def tile_list_introduction_scores_kernel(
    tc, tab_words, tab_scales, offs, pos1, pos2, w1, b1, w2_words, w2_scales,
    thr, dist, w3, b3, w4_words, w4_scales, out,
):
    nc = tc.nc
    with ExitStack() as ctx:
        keep = ctx.enter_context(tc.tile_pool(name="keep", bufs=1))
        ring = ctx.enter_context(tc.tile_pool(name="ring", bufs=4))
        psum = ctx.enter_context(tc.psum_pool(name="psum", bufs=1))

        def bank(b, name):
            return psum.tile([P, BANK], F32, name=name, tag="bank%d" % b)

        offs_sb = keep.tile([P, S // 16], U16, name="offs_sb")
        pos1_sb = keep.tile([P, M // 16], U16, name="pos1_sb")
        pos2_sb = keep.tile([P, M // 16], U16, name="pos2_sb")
        tab = [keep.tile([P, T], I32, name="tab%d" % a) for a in range(PASSES)]
        tab_sc = keep.tile([P, T // 4], I32, name="tab_sc")
        w2_raw = keep.tile([P, PASSES, H], I32, name="w2_raw")
        w2_sc_raw = keep.tile([P, H // 4], I32, name="w2_sc_raw")
        w1_raw = [keep.tile([P, PACK, H], F32, name="w1_raw%d" % a) for a in range(PASSES)]
        b1_sb = keep.tile([P, PACK], F32, name="b1_sb", tag="gate")
        thr_sb = keep.tile([P, PACK], F32, name="thr_sb")
        b3_sb = keep.tile([P, N_TILES], F32, name="b3_sb")
        w3_raw = keep.tile([P, PACK, N], F32, name="w3_raw")
        dist_sb = keep.tile([P, PACK, M], F32, name="dist_sb")
        w4_sb = keep.tile([P, N // 2], I32, name="w4_sb", align_bytes=64)
        w4_sc = keep.tile([P, N // 4], I32, name="w4_sc", align_bytes=64)

        nc.vector.memset(w2_sc_raw[:], 0)
        nc.vector.memset(tab_sc[:], 0)
        nc.vector.memset(w4_sc[:], 0)

        def load_scales(tile, scales, quads):
            passes = scales.shape[0]
            words = scales.bitcast(I32)
            for q in quads:
                nc.sync.dma_start(
                    out=tile[32 * q : 32 * q + ROWS * passes, :],
                    in_=words[:, ROWS * q : ROWS * (q + 1), :],
                )

        def load_table(a):
            nc.sync.dma_start(out=tab[a][:], in_=tab_words[a].rearrange("p t i -> p (t i)").bitcast(I32))

        load_table(0)
        nc.sync.dma_start(out=offs_sb[:], in_=offs)
        load_scales(tab_sc, tab_scales, (2, 3))
        load_scales(w2_sc_raw, w2_scales, (2, 3))
        load_scales(tab_sc, tab_scales, (0, 1))
        nc.sync.dma_start(out=w2_raw[:], in_=w2_words.rearrange("a p c i -> p a (c i)").bitcast(I32))
        load_scales(w2_sc_raw, w2_scales, (0, 1))
        load_table(1)
        load_table(2)
        for a in range(PASSES):
            nc.sync.dma_start(
                out=w1_raw[a][:], in_=w1[a * 512 : (a + 1) * 512, :].rearrange("(p j) c -> p j c", j=PACK)
            )
        nc.sync.dma_start(out=b1_sb[:], in_=b1.rearrange("(p t) -> p t", t=PACK))
        nc.sync.dma_start(out=pos2_sb[:], in_=pos2)
        nc.sync.dma_start(out=w3_raw[:], in_=w3.rearrange("(p j) n -> p j n", j=PACK))
        nc.sync.dma_start(out=pos1_sb[:], in_=pos1)
        nc.sync.dma_start(out=thr_sb[:], in_=thr.rearrange("(p t) -> p t", t=PACK))
        nc.sync.dma_start(out=dist_sb[:], in_=dist.rearrange("(p t) m -> p t m", t=PACK))
        nc.sync.dma_start(out=w4_sb[:], in_=w4_words[0].bitcast(I32))
        load_scales(w4_sc, w4_scales, range(QUADS))
        with nc.allow_non_contiguous_dma(reason="one bias value a partition"):
            nc.sync.dma_start(out=b3_sb[:], in_=b3.rearrange("(c p) -> p c", p=P))

        v = [[keep.tile([P, BANK], U32, name="v%d_%d" % (a, s), align_bytes=64) for s in range(HALVES)] for a in range(PASSES)]
        v_sc = [keep.tile([P, BANK], U8, name="v_sc%d" % s, align_bytes=64) for s in range(HALVES)]

        def gather_table(a):
            for s in range(HALVES):
                cols = offs_sb[:, s * BANK // 16 : (s + 1) * BANK // 16]
                nc.vector.tensor_copy(out=v[a][s][:], in_=tab[a][:].bitcast(U32).indirect(cols))


        gather_table(0)
        for s in range(HALVES):
            cols = offs_sb[:, s * BANK // 16 : (s + 1) * BANK // 16]
            nc.vector.tensor_copy(out=v_sc[s][:], in_=tab_sc[:].bitcast(U8).indirect(cols))

        w2_q = keep.tile([P, PASSES, H], I32, name="w2_q", align_bytes=64)
        w2_sc = keep.tile([P, H], U8, name="w2_sc", align_bytes=64)
        nc.vector.tensor_copy(
            out=w2_sc[:].rearrange("p (t m) -> p t m", t=PACK),
            in_=w2_sc_raw[:].bitcast(U8).rearrange("p (m t) -> p t m", t=PACK),
        )
        for a in range(PASSES):
            nc.vector.tensor_copy(
                out=w2_q[:, a, :].rearrange("p (t m) -> p m t", t=PACK),
                in_=w2_raw[:, a, :].rearrange("p (m t) -> p m t", t=PACK),
            )
        gather_table(1)
        gather_table(2)

        def first_stage(acc, codes, scales, t, s):
            for a in range(PASSES):
                nc.tensor.matmul_mx(
                    out=acc[:],
                    lhsT=codes(a, t),
                    lhsT_scale=scales(a, t),
                    rhs=v[a][s][:].bitcast(FP8X4),
                    rhs_scale=v_sc[s][ROWS * a :, :],
                    start=(a == 0),
                    stop=(a == PASSES - 1),
                )

        g = [keep.tile([P, S], F32, name="g%d" % t) for t in range(PACK)]
        for s in range(HALVES):
            for t in range(PACK):
                acc = bank(PACK * s + t, "g_acc")
                first_stage(
                    acc,
                    lambda a, t: w2_q[:, a, t * P : (t + 1) * P].bitcast(FP8X4),
                    lambda a, t: w2_sc[ROWS * a :, t * P : (t + 1) * P],
                    t, s,
                )
                nc.scalar.copy(out=g[t][:, s * BANK : (s + 1) * BANK], in_=acc[:])

        w1_bf = [
            [
                keep.tile([P, 2 * H], BF16, name="w1_bf%d_%d" % (a, u), tag="w1_bf%d_%d" % (a, u), align_bytes=64)
                for u in range(2)
            ]
            for a in range(PASSES)
        ]
        w1_q = [keep.tile([P, H], U32, name="w1_q%d" % a, align_bytes=64) for a in range(PASSES)]
        w1_sc = [keep.tile([P, H], U8, name="w1_sc%d" % a, align_bytes=64) for a in range(PASSES)]

        def w1_plane(a, lo, hi):
            if a == 1 and lo >= 2:
                return w1_sc[2][ROWS:, (lo - 2) * P : (hi - 2) * P]
            return w1_sc[a][:, lo * P : hi * P]

        def round_w1(a, u):
            dst = w1_bf[a][u][:].rearrange("p (e m j) -> p m j e", e=2, j=PACK)
            src = w1_raw[a][:].rearrange("p j (m u e) -> p u m j e", u=2, e=2)
            nc.vector.tensor_copy(out=dst, in_=src[:, u])

        def quantise_w1(a, lo, hi):
            nc.vector.quantize_mx(
                out=w1_q[a][:, lo * P : hi * P].bitcast(FP8X4),
                scales=w1_plane(a, lo, hi),
                in_=w1_bf[a][lo // 2][:, (lo % 2) * H : (lo % 2 + hi - lo) * H],
            )

        h = [keep.tile([P, S], F32, name="h%d" % t) for t in range(PACK)]

        def make_h(t):
            for s in range(HALVES):
                acc = bank(HALVES * t + s, "h_acc")
                first_stage(
                    acc,
                    lambda a, t: w1_q[a][:, t * P : (t + 1) * P].bitcast(FP8X4),
                    lambda a, t: w1_plane(a, t, t + 1),
                    t, s,
                )
                nc.scalar.activation(
                    out=h[t][:, s * BANK : (s + 1) * BANK], in_=acc[:], func=ACT.Silu, bias=b1_sb[:, t : t + 1]
                )

        round_w1(0, 0)
        round_w1(0, 1)
        quantise_w1(0, 0, 2)
        quantise_w1(0, 2, 4)
        round_w1(1, 0)
        round_w1(1, 1)
        quantise_w1(1, 0, 2)
        round_w1(2, 0)
        quantise_w1(2, 0, 1)
        quantise_w1(2, 1, 2)
        round_w1(2, 1)
        for t in range(2):
            make_h(t)
            quantise_w1(2, t + 2, t + 3)
            quantise_w1(1, t + 2, t + 3)
        make_h(2)
        make_h(3)

        picked = keep.tile([P, PACK, M], F32, name="picked", tag="w1_bf1_1", align_bytes=64)
        for t in range(PACK):
            nc.vector.tensor_copy(out=picked[:, t, :], in_=g[t][:].indirect(pos2_sb[:]))

        w3_bf = keep.tile([P, N * PACK], BF16, name="w3_bf", align_bytes=64)
        w3_q = keep.tile([P, N], U32, name="w3_q", align_bytes=64)
        w3_sc = keep.tile([P, N], U8, name="w3_sc", align_bytes=64)
        nc.vector.tensor_copy(
            out=w3_bf[:].rearrange("p (c i j) -> p c j i", i=4, j=PACK),
            in_=w3_raw[:].rearrange("p j (c i) -> p c j i", i=4),
        )
        for u in range(2):
            nc.vector.quantize_mx(
                out=w3_q[:, u * N // 2 : (u + 1) * N // 2].bitcast(FP8X4),
                scales=w3_sc[:, u * N // 2 : (u + 1) * N // 2],
                in_=w3_bf[:, u * N * 2 : (u + 1) * N * 2],
            )

        gate = keep.tile([P, PACK, M], F32, name="gate", tag="gate")
        for c in range(CHUNKS):
            cols = slice(c * CHUNK, (c + 1) * CHUNK)
            for t in range(PACK):
                nc.scalar.activation(
                    out=gate[:, t, cols],
                    in_=h[t][:].indirect(pos1_sb[:, c * CHUNK // 16 : (c + 1) * CHUNK // 16]),
                    func=ACT.Sigmoid,
                    bias=thr_sb[:, t : t + 1],
                )
        x_qs, x_scs = [], []
        prod = keep.tile([P, PACK, CHUNK], F32, name="prod")
        for c in range(CHUNKS):
            cols = slice(c * CHUNK, (c + 1) * CHUNK)
            for t in range(PACK - 1):
                nc.vector.tensor_tensor(out=prod[:, t, :], in0=gate[:, t, cols], in1=dist_sb[:, t, cols], op=ALU.mult)
            x_bf = keep.tile([P, CHUNK * PACK], BF16, name="x_bf%d" % c, align_bytes=64)
            x_q = keep.tile([P, CHUNK], U32, name="x_q%d" % c, align_bytes=64)
            x_sc = keep.tile([P, CHUNK], U8, name="x_sc%d" % c, align_bytes=64)
            parts = [slice(c * CHUNK + d * P, c * CHUNK + (d + 1) * P) for d in range(2)]
            for d, part in enumerate(parts):
                nc.vector.tensor_tensor(
                    out=prod[:, PACK - 1, d * P : (d + 1) * P],
                    in0=gate[:, PACK - 1, part],
                    in1=dist_sb[:, PACK - 1, part],
                    op=ALU.mult,
                )
            for d, part in enumerate(parts):
                nc.vector.tensor_tensor(
                    out=x_bf[:, d * P * PACK : (d + 1) * P * PACK].rearrange("p (c i t) -> p c t i", i=2, t=PACK),
                    in0=prod[:, :, d * P : (d + 1) * P].rearrange("p t (c i) -> p c t i", i=2),
                    in1=picked[:, :, part].rearrange("p t (c i) -> p c t i", i=2),
                    op=ALU.add,
                )
            for d in range(2):
                nc.vector.quantize_mx(
                    out=x_q[:, d * P : (d + 1) * P].bitcast(FP8X4),
                    scales=x_sc[:, d * P : (d + 1) * P],
                    in_=x_bf[:, d * P * PACK : (d + 1) * P * PACK],
                )
            x_qs.append(x_q)
            x_scs.append(x_sc)

        for c in range(CHUNKS):
            cols = slice(c * CHUNK, (c + 1) * CHUNK)
            x_q, x_sc = x_qs[c], x_scs[c]
            y3s, y4s = [], []
            for pair in range(PAIRS):
                y3s.append(bank((c * PAIRS + pair) % 4, "y3"))
                y4s.append(bank(4 + (c * PAIRS + pair) % 4, "y4"))

            def product3(pair):
                for e in range(2):
                    n = 2 * pair + e
                    nc.tensor.matmul_mx(
                        out=y3s[pair][:, e * CHUNK : (e + 1) * CHUNK],
                        lhsT=w3_q[:, n * P : (n + 1) * P].bitcast(FP8X4),
                        lhsT_scale=w3_sc[:, n * P : (n + 1) * P],
                        rhs=x_q[:].bitcast(FP8X4),
                        rhs_scale=x_sc[:],
                        start=True,
                        stop=True,
                    )

            def product4(pair):
                for e in range(2):
                    n = 2 * pair + e
                    nc.tensor.matmul_mx(
                        out=y4s[pair][:, e * CHUNK : (e + 1) * CHUNK],
                        lhsT=w4_sb[:].bitcast(U8)[:, 2 * n * P : 2 * (n + 1) * P].bitcast(FP4X4),
                        lhsT_scale=w4_sc[:].bitcast(U8)[:, n * P : (n + 1) * P],
                        rhs=x_q[:].bitcast(FP8X4),
                        rhs_scale=x_sc[:],
                        start=True,
                        stop=True,
                    )

            product3(0)
            for pair in range(PAIRS):
                if pair + 1 < PAIRS:
                    product3(pair + 1)
                product4(pair)
            for pair in range(PAIRS):
                y3_sb = ring.tile([P, BANK], F32, name="y3_sb")
                for e in range(2):
                    n = 2 * pair + e
                    nc.scalar.activation(
                        out=y3_sb[:, e * CHUNK : (e + 1) * CHUNK],
                        in_=y3s[pair][:, e * CHUNK : (e + 1) * CHUNK],
                        func=ACT.Identity,
                        bias=b3_sb[:, n : n + 1],
                    )
                best = ring.tile([P, BANK], F32, name="best", bufs=6)
                nc.vector.tensor_tensor(out=best[:], in0=y4s[pair][:], in1=y3_sb[:], op=ALU.max)
                nc.sync.dma_start(
                    out=out[2 * pair * P : 2 * (pair + 1) * P, cols].rearrange("(e p) m -> p e m", p=P),
                    in_=best[:].rearrange("p (e m) -> p e m", e=2),
                )
